import numpy as np
import ml_dtypes


def mxq(x, axis, fmt="e4m3"):
    dtype, down = {"e4m3": (ml_dtypes.float8_e4m3fn, 7), "e5m2": (ml_dtypes.float8_e5m2, 14)}[fmt]
    v = np.moveaxis(np.asarray(x, np.float32).astype(ml_dtypes.bfloat16).astype(np.float64), axis, -1)
    blocks = v.reshape(v.shape[:-1] + (-1, 32))
    amax = np.abs(blocks).max(-1, keepdims=True)
    byte = np.maximum(np.where(amax > 0, np.frexp(amax)[1] - 1 + 127, 0) - down, 1)
    scale = np.exp2(byte - 127.0)
    codes = (blocks / scale).astype(np.float32).astype(dtype).astype(np.float64)
    return np.moveaxis((codes * scale).reshape(v.shape), -1, axis)


WIDE = False


def mx_kscale(k):
    if not WIDE:
        return np.ones(k)
    levels = np.array([10, -10, 5, -5, 0])
    if k % 512:
        return np.exp2(np.random.permutation(np.resize(levels, k // 32))).repeat(32)
    a = np.empty((k // 512, 16))
    for p in range(k // 512):
        a[p, :8] = np.random.permutation(np.resize(levels, 8))
        for g in range(8):
            far = levels[np.abs(levels - a[p, g]) >= 10]
            a[p, g + 8] = far[np.random.randint(len(far))]
    return np.exp2(a.ravel()).repeat(32)


def f64(x):
    return np.asarray(x).astype(np.float64)


def striped(idx):
    return np.tile(idx.reshape(-1, 16).T, (8, 1)).astype(np.uint16)


def unstriped(offs):
    return offs[:16].T.reshape(-1).astype(np.int64)


E2M1 = np.array([0.0, 0.5, 1.0, 1.5, 2.0, 3.0, 4.0, 6.0, -0.0, -0.5, -1.0, -1.5, -2.0, -3.0, -4.0, -6.0])


def pack_weight(w, fmt):
    k, n = w.shape
    w = f64(np.asarray(w, np.float32).astype(ml_dtypes.bfloat16)).reshape(k // 32, 32, n)
    amax = np.abs(w).max(1)
    if fmt == "e4m3":
        byte = np.frexp(amax)[1] - 1 + 127 - 7
    else:
        mant, ex = np.frexp(amax / 6.0)
        byte = np.where(mant > 0.5, ex, ex - 1) + 127
    byte = np.clip(np.where(amax > 0, byte, 1), 1, 254)
    scaled = (w * np.exp2(127.0 - byte)[:, None, :]).reshape(k, n).astype(np.float32)
    by_word = np.ascontiguousarray(scaled.reshape(k // 512, 128, 4, n).transpose(0, 1, 3, 2))
    if fmt == "e4m3":
        words = by_word.astype(ml_dtypes.float8_e4m3fn).view(np.uint8)
    else:
        c = by_word.astype(ml_dtypes.float4_e2m1fn).view(np.uint8) & 0xF
        words = (c[..., 0::2] | (c[..., 1::2] << 4)).reshape(k // 512, 128, 2 * n)
    return np.ascontiguousarray(words), np.ascontiguousarray(byte.astype(np.uint8).reshape(k // 512, 16, n))


def unpack_weight(words, scales, fmt):
    g, _, n = scales.shape
    words = np.ascontiguousarray(words).reshape(g, 128, n, -1)
    if fmt == "e4m3":
        vals = words.view(ml_dtypes.float8_e4m3fn).astype(np.float64)
    else:
        nib = np.empty((g, 128, n, 4), np.uint8)
        nib[..., 0::2] = words & 0xF
        nib[..., 1::2] = words >> 4
        vals = E2M1[nib]
    vals = vals * np.repeat(np.exp2(scales.astype(np.float64) - 127.0), 8, axis=1)[..., None]
    return vals.transpose(0, 1, 3, 2).reshape(g * 512, n)


def relu2(v):
    return np.maximum(v, 0.0) ** 2


K, T, E, C, H, N = 1024, 1280, 10, 128, 512, 128


def by_expert(wq, xq):
    return np.concatenate([wq[e].T @ xq[:, e * C:(e + 1) * C] for e in range(E)], axis=1)


def setup_inputs():
    n = np.random.standard_normal
    s = mx_kscale(K)
    u = mx_kscale(H)
    slot_token = np.random.permutation(T)[:E * C]
    x = pack_weight(n((K, T)) * s[:, None], "e4m3")
    w2 = pack_weight(n((H, N)) / np.sqrt(H) / u[:, None] ** 2, "e2m1")
    return {
        "x_words": x[0],
        "x_scales": x[1],
        "w1": (n((E, K, H)) / np.sqrt(K) / s[None, :, None] * u).astype(np.float32),
        "w2_words": w2[0],
        "w2_scales": w2[1],
        "gate": np.tile(np.random.uniform(0.2, 1.0, E * C), (128, 1)).astype(np.float32),
        "offs": striped(slot_token),
    }


def reference(x_words, x_scales, w1, w2_words, w2_scales, gate, offs):
    w1q = mxq(f64(w1), 1, "e4m3")
    w2 = unpack_weight(w2_words, w2_scales, "e2m1")
    idx = unstriped(offs)
    xq = unpack_weight(x_words, x_scales, "e4m3")[:, idx]
    h = relu2(by_expert(w1q, xq))
    c = np.zeros((H, T))
    c[:, idx] = f64(gate[:1]) * h
    return w2.T @ mxq(c, 0, "e4m3")

@@ -1,0 +1,204 @@
+from contextlib import ExitStack
+
+import concourse.mybir as mybir
+from concourse.masks import make_identity
+
+K, T, E, C, H, N = 1024, 1280, 10, 128, 512, 128
+FLOPS = 2 * T * (K * H + H * N)
+
+F32 = mybir.dt.float32
+BF16 = mybir.dt.bfloat16
+I32 = mybir.dt.int32
+U32 = mybir.dt.uint32
+U16 = mybir.dt.uint16
+U8 = mybir.dt.uint8
+FP8X4 = mybir.dt.float8_e4m3fn_x4
+FP4X4 = mybir.dt.float4_e2m1fn_x4
+MULT = mybir.AluOpType.mult
+MAX = mybir.AluOpType.max
+COPY = mybir.ActivationFunctionType.Copy
+
+P = 128
+PACK = 4
+K_PASS = P * PACK
+PASSES = K // K_PASS
+PER_COLUMN = 16
+GATHER = 640
+SCATTER = 256
+TOKEN_CHUNKS = ((0, 512), (512, 1024), (1024, 1280))
+VECTOR_COLUMNS = 136
+VECTOR_COLUMNS_LAST = 320
+SCALAR_ALONE = 2
+
+
+def tile_moe_sdn_lin_relu2_kernel(
+    tc, x_words, x_scales, w1, w2_words, w2_scales, gate, offs, out
+):
+    nc = tc.nc
+    with ExitStack() as ctx:
+        keep = ctx.enter_context(tc.tile_pool(name="keep", bufs=1))
+        loads = ctx.enter_context(tc.tile_pool(name="loads", bufs=14))
+        work = ctx.enter_context(tc.tile_pool(name="work", bufs=4))
+        psum = ctx.enter_context(tc.psum_pool(name="psum", bufs=3))
+
+        def listed(a, b):
+            return offsets[:, a // PER_COLUMN : b // PER_COLUMN]
+
+        token_scales = keep.tile([P, T], U8, align_bytes=64)
+        nc.vector.memset(token_scales[:].bitcast(I32), 0)
+        w2_plane = keep.tile([P, N], U8, align_bytes=64)
+        nc.vector.memset(w2_plane[:].bitcast(I32), 0)
+        gate_rows = keep.tile([P, C], F32)
+        nc.gpsimd.memset(gate_rows[:], 0.0)
+        identity = keep.tile([P, P], F32)
+        make_identity(nc, identity[:])
+
+        offsets = keep.tile([P, T // PER_COLUMN], U16, name="offsets")
+        nc.sync.dma_start(offsets[:], offs)
+        token_words = [keep.tile([P, T], U32, name="token_words%d" % s, align_bytes=64) for s in range(PASSES)]
+        nc.sync.dma_start(
+            token_words[0][:].bitcast(I32), x_words[0].rearrange("p t d -> p (t d)").bitcast(I32)
+        )
+        for q in range(4):
+            nc.sync.dma_start(
+                token_scales[32 * q : 32 * q + 4 * PASSES, :].bitcast(I32),
+                x_scales[:, 4 * q : 4 * q + 4, :].bitcast(I32),
+            )
+        nc.sync.dma_start(
+            token_words[1][:].bitcast(I32), x_words[1].rearrange("p t d -> p (t d)").bitcast(I32)
+        )
+
+        nc.scalar.dma_start(gate_rows[0:E, :], gate[0].rearrange("(e u) -> e u", u=C))
+        gate_turned = psum.tile([P, 2, 2 * C], F32, tag="turned")
+        nc.tensor.transpose(gate_turned[:, 0, :C], gate_rows[:], identity[:])
+        slot_gate = keep.tile([P, 16], F32)
+        nc.scalar.copy(slot_gate[:], gate_turned[:, 0, 0:16])
+
+        slot_words = [keep.tile([P, T], U32, name="slot_words%d" % s, align_bytes=64) for s in range(PASSES)]
+        slot_scales = keep.tile([P, T], U8, align_bytes=64)
+        token_pairs = [keep.tile([P, T], F32, name="token_pairs%d" % u) for u in range(2)]
+        w2_codes = keep.tile([P, 2 * N], U8, align_bytes=64)
+        spare = keep.tile([P, 2, H], F32)
+
+        for a in range(0, T, GATHER):
+            b = a + GATHER
+            nc.vector.tensor_copy(slot_words[0][:, a:b], token_words[0][:].indirect(listed(a, b)))
+            nc.vector.tensor_copy(slot_scales[:, a:b], token_scales[:].indirect(listed(a, b)))
+            nc.vector.tensor_copy(slot_words[1][:, a:b], token_words[1][:].indirect(listed(a, b)))
+
+        sums = {}
+        turned = {}
+
+        def activate(e, room):
+            gated = room[:, 0:2, H // 2 :]
+            nc.scalar.activation(
+                gated, sums[e][:].rearrange("p (a h) -> p a h", a=2), COPY, scale=slot_gate[:, e : e + 1]
+            )
+            hidden = work.tile([P, H], BF16)
+            nc.vector.scalar_tensor_tensor(
+                hidden[:].rearrange("p (a h) -> p a h", a=2),
+                sums[e][:].rearrange("p (a h) -> p a h", a=2),
+                0.0,
+                gated,
+                MAX,
+                MULT,
+            )
+            pairs = hidden[:].bitcast(F32)
+            if e % 2 == 0:
+                turned[e // 2] = psum.tile([P, 2, 2 * C], F32, tag="turned", name="turned")
+            for u in range(2):
+                nc.tensor.transpose(
+                    turned[e // 2][:, u, (e % 2) * C : (e % 2 + 1) * C], pairs[:, u : H // 2 : 2], identity[:]
+                )
+
+        def send_back(g, u, staged):
+            nc.scalar.copy(staged, turned[g][:, u, :])
+            nc.vector.tensor_copy(token_pairs[u][:].indirect(listed(g * SCATTER, (g + 1) * SCATTER)), staged)
+
+        for step in range(E * PASSES):
+            e, s = divmod(step, PASSES)
+            slots = slice(e * C, (e + 1) * C)
+            if step == 4:
+                nc.sync.dma_start(w2_codes[:].bitcast(I32), w2_words[0].bitcast(I32))
+                for q in range(4):
+                    nc.sync.dma_start(
+                        w2_plane[32 * q : 32 * q + 4, :].bitcast(I32),
+                        w2_scales[0, 4 * q : 4 * q + 4, :].bitcast(I32),
+                    )
+            raw = loads.tile([P, PACK, H], F32)
+            nc.sync.dma_start(
+                raw[:], w1[e, s * K_PASS : (s + 1) * K_PASS, :].rearrange("(p j) h -> p j h", j=PACK)
+            )
+            grouped = work.tile([P, H, PACK], BF16, align_bytes=64)
+            dst = grouped[:].rearrange("p (c i) j -> p c j i", i=4)
+            src = raw[:].rearrange("p j (c i) -> p c j i", i=4)
+            if step < SCALAR_ALONE:
+                cut = 0
+            elif step < E * PASSES - 1:
+                cut = VECTOR_COLUMNS // 4
+            else:
+                cut = VECTOR_COLUMNS_LAST // 4
+            nc.scalar.copy(dst[:, cut:], src[:, cut:])
+            if cut:
+                nc.vector.tensor_copy(dst[:, :cut], src[:, :cut])
+            codes = work.tile([P, H], U32, align_bytes=64)
+            scales = work.tile([P, H], U8, align_bytes=64)
+            nc.vector.quantize_mx(
+                out=codes[:].bitcast(FP8X4), scales=scales[:], in_=grouped[:].rearrange("p h j -> p (h j)")
+            )
+            if s == 0:
+                sums[e] = psum.tile([P, H], F32, tag="sums", name="sums")
+            nc.tensor.matmul_mx(
+                out=sums[e][:],
+                lhsT=slot_words[s][:, slots].bitcast(FP8X4),
+                lhsT_scale=slot_scales[4 * s : P, slots],
+                rhs=codes[:].bitcast(FP8X4),
+                rhs_scale=scales[:],
+                start=(s == 0),
+                stop=(s == PASSES - 1),
+            )
+            if s == 0 and e >= 1:
+                activate(e - 1, raw)
+            if s == 1 and e >= 2:
+                send_back(e // 2 - 1, e % 2, raw[:, 0, H // 2 :])
+
+        activate(E - 1, spare)
+        for u in range(2):
+            send_back(E // 2 - 1, u, spare[:, u, : H // 2])
+
+        both = [keep.tile([P, 2, b - a], F32, name="both%d" % a) for a, b in TOKEN_CHUNKS]
+        for i, (a, b) in enumerate(TOKEN_CHUNKS):
+            nc.scalar.copy(both[i][:, 0, :], token_pairs[0][:, a:b])
+        for i, (a, b) in enumerate(TOKEN_CHUNKS):
+            if i == 1:
+                nc.scalar.copy(both[i][:, 1, :], token_pairs[1][:, a:b])
+            else:
+                nc.vector.tensor_copy(both[i][:, 1, :], token_pairs[1][:, a:b])
+        quads = [keep.tile([P, PACK * (b - a)], BF16, name="quads%d" % a, align_bytes=64) for a, b in TOKEN_CHUNKS]
+        for i, (a, b) in enumerate(TOKEN_CHUNKS):
+            dst = quads[i][:].bitcast(F32).rearrange("p (t u) -> p t u", u=2)
+            src = both[i][:].rearrange("p u t -> p t u")
+            if i == 1:
+                nc.scalar.copy(dst, src)
+            else:
+                nc.vector.tensor_copy(dst, src)
+        for i, (a, b) in enumerate(TOKEN_CHUNKS):
+            c_codes = keep.tile([P, b - a], U32, name="c_codes%d" % a, align_bytes=64)
+            c_scales = keep.tile([P, b - a], U8, name="c_scales%d" % a, align_bytes=64)
+            nc.vector.quantize_mx(out=c_codes[:].bitcast(FP8X4), scales=c_scales[:], in_=quads[i][:])
+            product = psum.tile([P, H], F32, tag="sums")
+            nc.tensor.matmul_mx(
+                out=product[:, : b - a],
+                lhsT=w2_codes[:].bitcast(FP4X4),
+                lhsT_scale=w2_plane[:],
+                rhs=c_codes[:].bitcast(FP8X4),
+                rhs_scale=c_scales[:],
+                start=True,
+                stop=True,
+            )
+            result = keep.tile([P, b - a], F32, name="result%d" % a)
+            if i == 2:
+                nc.vector.tensor_copy(result[:], product[:, : b - a])
+            else:
+                nc.scalar.copy(result[:], product[:, : b - a])
+            nc.sync.dma_start(out[:, a:b], result[:])

@@ -15,6 +15,7 @@ U8 = mybir.dt.uint8
 FP8X4 = mybir.dt.float8_e4m3fn_x4
 FP4X4 = mybir.dt.float4_e2m1fn_x4
 MULT = mybir.AluOpType.mult
+ADD = mybir.AluOpType.add
 MAX = mybir.AluOpType.max
 COPY = mybir.ActivationFunctionType.Copy
 
@@ -22,13 +23,21 @@ P = 128
 PACK = 4
 K_PASS = P * PACK
 PASSES = K // K_PASS
+QUADRANT = 32
+HALF = H // 2
 PER_COLUMN = 16
-GATHER = 640
-SCATTER = 256
-TOKEN_CHUNKS = ((0, 512), (512, 1024), (1024, 1280))
-VECTOR_COLUMNS = 136
-VECTOR_COLUMNS_LAST = 320
-SCALAR_ALONE = 2
+BANK = 512
+
+GATHER = T // 2
+BANK_STARTS = (0, 2, 6)
+SCATTERS = ((0, 256), (256, 448), (448, 608), (608, 768), (768, 960), (960, 1120), (1120, 1280))
+GPSIMD_COLUMNS = 128
+TOKEN_CHUNKS = ((0, 512), (512, 768), (768, 1024), (1024, 1280))
+VECTOR_CHUNKS = 2
+
+
+def activation_step(e):
+    return PASSES * e + (3 if e < E - 3 else 2)
 
 
 def tile_moe_sdn_lin_relu2_kernel(
@@ -39,10 +48,8 @@ def tile_moe_sdn_lin_relu2_kernel(
         keep = ctx.enter_context(tc.tile_pool(name="keep", bufs=1))
         loads = ctx.enter_context(tc.tile_pool(name="loads", bufs=14))
         work = ctx.enter_context(tc.tile_pool(name="work", bufs=4))
-        psum = ctx.enter_context(tc.psum_pool(name="psum", bufs=3))
-
-        def listed(a, b):
-            return offsets[:, a // PER_COLUMN : b // PER_COLUMN]
+        psum_sums = ctx.enter_context(tc.psum_pool(name="psum_sums", bufs=4))
+        psum_pairs = ctx.enter_context(tc.psum_pool(name="psum_pairs", bufs=2))
 
         token_scales = keep.tile([P, T], U8, align_bytes=64)
         nc.vector.memset(token_scales[:].bitcast(I32), 0)
@@ -55,122 +62,140 @@ def tile_moe_sdn_lin_relu2_kernel(
 
         offsets = keep.tile([P, T // PER_COLUMN], U16, name="offsets")
         nc.sync.dma_start(offsets[:], offs)
+
+        def listed(a, b):
+            return offsets[:, a // PER_COLUMN : b // PER_COLUMN]
+
         token_words = [keep.tile([P, T], U32, name="token_words%d" % s, align_bytes=64) for s in range(PASSES)]
-        nc.sync.dma_start(
-            token_words[0][:].bitcast(I32), x_words[0].rearrange("p t d -> p (t d)").bitcast(I32)
-        )
-        for q in range(4):
+        nc.sync.dma_start(token_words[0][:].bitcast(I32), x_words[0].rearrange("p t d -> p (t d)").bitcast(I32))
+        for q in range(P // QUADRANT):
             nc.sync.dma_start(
-                token_scales[32 * q : 32 * q + 4 * PASSES, :].bitcast(I32),
+                token_scales[QUADRANT * q : QUADRANT * q + 4 * PASSES, :].bitcast(I32),
                 x_scales[:, 4 * q : 4 * q + 4, :].bitcast(I32),
             )
-        nc.sync.dma_start(
-            token_words[1][:].bitcast(I32), x_words[1].rearrange("p t d -> p (t d)").bitcast(I32)
-        )
+        nc.sync.dma_start(token_words[1][:].bitcast(I32), x_words[1].rearrange("p t d -> p (t d)").bitcast(I32))
 
         nc.scalar.dma_start(gate_rows[0:E, :], gate[0].rearrange("(e u) -> e u", u=C))
-        gate_turned = psum.tile([P, 2, 2 * C], F32, tag="turned")
-        nc.tensor.transpose(gate_turned[:, 0, :C], gate_rows[:], identity[:])
-        slot_gate = keep.tile([P, 16], F32)
-        nc.scalar.copy(slot_gate[:], gate_turned[:, 0, 0:16])
+        gate_turned = psum_pairs.tile([P, BANK], F32, tag="pairs0")
+        nc.tensor.transpose(gate_turned[:, :P], gate_rows[:], identity[:])
+        slot_gate = keep.tile([P, SCATTERS[-2][1] - SCATTERS[-2][0]], F32)
+        nc.scalar.copy(slot_gate[:, :16], gate_turned[:, :16])
 
         slot_words = [keep.tile([P, T], U32, name="slot_words%d" % s, align_bytes=64) for s in range(PASSES)]
         slot_scales = keep.tile([P, T], U8, align_bytes=64)
-        token_pairs = [keep.tile([P, T], F32, name="token_pairs%d" % u) for u in range(2)]
-        w2_codes = keep.tile([P, 2 * N], U8, align_bytes=64)
-        spare = keep.tile([P, 2, H], F32)
-
         for a in range(0, T, GATHER):
             b = a + GATHER
             nc.vector.tensor_copy(slot_words[0][:, a:b], token_words[0][:].indirect(listed(a, b)))
             nc.vector.tensor_copy(slot_scales[:, a:b], token_scales[:].indirect(listed(a, b)))
             nc.vector.tensor_copy(slot_words[1][:, a:b], token_words[1][:].indirect(listed(a, b)))
 
+        token_pairs = [keep.tile([P, T], F32, name="token_pairs%d" % u) for u in range(2)]
+        w2_codes = keep.tile([P, 2 * N], U8, align_bytes=64)
+        spare = keep.tile([P, 2, H], F32)
         sums = {}
+        hidden = {}
         turned = {}
 
-        def activate(e, room):
-            gated = room[:, 0:2, H // 2 :]
-            nc.scalar.activation(
-                gated, sums[e][:].rearrange("p (a h) -> p a h", a=2), COPY, scale=slot_gate[:, e : e + 1]
-            )
-            hidden = work.tile([P, H], BF16)
-            nc.vector.scalar_tensor_tensor(
-                hidden[:].rearrange("p (a h) -> p a h", a=2),
-                sums[e][:].rearrange("p (a h) -> p a h", a=2),
-                0.0,
-                gated,
-                MAX,
-                MULT,
-            )
-            pairs = hidden[:].bitcast(F32)
-            if e % 2 == 0:
-                turned[e // 2] = psum.tile([P, 2, 2 * C], F32, tag="turned", name="turned")
-            for u in range(2):
-                nc.tensor.transpose(
-                    turned[e // 2][:, u, (e % 2) * C : (e % 2 + 1) * C], pairs[:, u : H // 2 : 2], identity[:]
-                )
+        def bank_start(e):
+            return max(f for f in BANK_STARTS if f <= e)
 
-        def send_back(g, u, staged):
-            nc.scalar.copy(staged, turned[g][:, u, :])
-            nc.vector.tensor_copy(token_pairs[u][:].indirect(listed(g * SCATTER, (g + 1) * SCATTER)), staged)
-
-        for step in range(E * PASSES):
-            e, s = divmod(step, PASSES)
+        def multiply(e, s, a, b):
             slots = slice(e * C, (e + 1) * C)
-            if step == 4:
-                nc.sync.dma_start(w2_codes[:].bitcast(I32), w2_words[0].bitcast(I32))
-                for q in range(4):
-                    nc.sync.dma_start(
-                        w2_plane[32 * q : 32 * q + 4, :].bitcast(I32),
-                        w2_scales[0, 4 * q : 4 * q + 4, :].bitcast(I32),
-                    )
-            raw = loads.tile([P, PACK, H], F32)
+            raw = loads.tile([P, PACK, b - a], F32)
             nc.sync.dma_start(
-                raw[:], w1[e, s * K_PASS : (s + 1) * K_PASS, :].rearrange("(p j) h -> p j h", j=PACK)
+                raw[:], w1[e, s * K_PASS : (s + 1) * K_PASS, a:b].rearrange("(p j) h -> p j h", j=PACK)
             )
-            grouped = work.tile([P, H, PACK], BF16, align_bytes=64)
-            dst = grouped[:].rearrange("p (c i) j -> p c j i", i=4)
-            src = raw[:].rearrange("p j (c i) -> p c j i", i=4)
-            if step < SCALAR_ALONE:
-                cut = 0
-            elif step < E * PASSES - 1:
-                cut = VECTOR_COLUMNS // 4
-            else:
-                cut = VECTOR_COLUMNS_LAST // 4
-            nc.scalar.copy(dst[:, cut:], src[:, cut:])
-            if cut:
-                nc.vector.tensor_copy(dst[:, :cut], src[:, :cut])
-            codes = work.tile([P, H], U32, align_bytes=64)
-            scales = work.tile([P, H], U8, align_bytes=64)
+            grouped = work.tile([P, b - a, PACK], BF16, align_bytes=64)
+            cut = GPSIMD_COLUMNS * (b - a) // H
+            nc.scalar.copy(
+                grouped[:, cut:, :].rearrange("p (c i) j -> p c j i", i=4),
+                raw[:, :, cut:].rearrange("p j (c i) -> p c j i", i=4),
+            )
+            nc.gpsimd.tensor_scalar(
+                grouped[:, :cut, :], raw[:, :, :cut].rearrange("p j h -> p h j"), 1.0, 0.0, MULT, ADD
+            )
+            codes = work.tile([P, b - a], U32, align_bytes=64)
+            scales = work.tile([P, b - a], U8, align_bytes=64)
             nc.vector.quantize_mx(
                 out=codes[:].bitcast(FP8X4), scales=scales[:], in_=grouped[:].rearrange("p h j -> p (h j)")
             )
-            if s == 0:
-                sums[e] = psum.tile([P, H], F32, tag="sums", name="sums")
-            nc.tensor.matmul_mx(
-                out=sums[e][:],
-                lhsT=slot_words[s][:, slots].bitcast(FP8X4),
-                lhsT_scale=slot_scales[4 * s : P, slots],
-                rhs=codes[:].bitcast(FP8X4),
-                rhs_scale=scales[:],
-                start=(s == 0),
-                stop=(s == PASSES - 1),
-            )
-            if s == 0 and e >= 1:
-                activate(e - 1, raw)
-            if s == 1 and e >= 2:
-                send_back(e // 2 - 1, e % 2, raw[:, 0, H // 2 :])
+            width = H if e < E - 1 else HALF
+            for c in range(a, b, width):
+                if s == 0:
+                    sums[e, c] = psum_sums.tile([P, BANK], F32, tag="sums", name="sums")
+                nc.tensor.matmul_mx(
+                    out=sums[e, c][:, :width],
+                    lhsT=slot_words[s][:, slots].bitcast(FP8X4),
+                    lhsT_scale=slot_scales[4 * s : P, slots],
+                    rhs=codes[:, c - a : c - a + width].bitcast(FP8X4),
+                    rhs_scale=scales[:, c - a : c - a + width],
+                    start=(s == 0),
+                    stop=(s == PASSES - 1),
+                )
+            return raw
 
-        activate(E - 1, spare)
+        def activate(e, a, b, gated):
+            v = sums[e, a][:, : b - a].rearrange("p (r h) -> p r h", h=HALF)
+            nc.scalar.activation(gated, v, COPY, scale=slot_gate[:, e : e + 1])
+            nc.vector.scalar_tensor_tensor(
+                hidden[e][:, a:b].rearrange("p (r h) -> p r h", h=HALF), v, 0.0, gated, MAX, MULT
+            )
+
+        def turn(e):
+            first = bank_start(e)
+            pairs = hidden[e][:].bitcast(F32)
+            for u in range(2):
+                if e == first:
+                    turned[first, u] = psum_pairs.tile([P, BANK], F32, tag="pairs%d" % u, name="turned")
+                nc.tensor.transpose(
+                    turned[first, u][:, (e - first) * C : (e - first + 1) * C], pairs[:, u:HALF:2], identity[:]
+                )
+
+        def send_back(e, u, room):
+            first = bank_start(e)
+            for a, b in SCATTERS:
+                if e * C < b <= (e + 1) * C:
+                    staged = room[:, room.shape[1] - (b - a) :]
+                    nc.scalar.copy(staged, turned[first, u][:, a - first * C : b - first * C])
+                    nc.vector.tensor_copy(token_pairs[u][:].indirect(listed(a, b)), staged)
+
+        last = E - 1
+        pieces = [(e, s, 0, H) for e in range(E) for s in range(PASSES)][:-1]
+        pieces.extend([(last, PASSES - 1, 0, HALF), (last, PASSES - 1, HALF, H)])
+        for step, piece in enumerate(pieces):
+            if step == 4:
+                nc.sync.dma_start(w2_codes[:].bitcast(I32), w2_words[0].bitcast(I32))
+                for q in range(P // QUADRANT):
+                    nc.sync.dma_start(
+                        w2_plane[QUADRANT * q : QUADRANT * q + 4, :].bitcast(I32),
+                        w2_scales[0, 4 * q : 4 * q + 4, :].bitcast(I32),
+                    )
+            spent = multiply(*piece)
+            due = [e for e in range(last) if activation_step(e) == step]
+            for e in due:
+                hidden[e] = work.tile([P, H], BF16, name="hidden")
+                activate(e, 0, H, spent[:, 0:2, HALF:])
+            for e in range(last - 1):
+                for u in range(2):
+                    if activation_step(e) + 1 + u == step:
+                        send_back(e, u, spent[:, 2 + u, :])
+            for e in due:
+                turn(e)
+
+        hidden[last] = work.tile([P, H], BF16, name="hidden")
+        for r in range(2):
+            activate(last, r * HALF, (r + 1) * HALF, spare[:, r : r + 1, HALF:])
+        send_back(last - 1, 0, spent[:, 0, :])
+        send_back(last - 1, 1, slot_gate[:])
+        turn(last)
         for u in range(2):
-            send_back(E // 2 - 1, u, spare[:, u, : H // 2])
+            send_back(last, u, spare[:, u, :HALF])
 
         both = [keep.tile([P, 2, b - a], F32, name="both%d" % a) for a, b in TOKEN_CHUNKS]
         for i, (a, b) in enumerate(TOKEN_CHUNKS):
             nc.scalar.copy(both[i][:, 0, :], token_pairs[0][:, a:b])
         for i, (a, b) in enumerate(TOKEN_CHUNKS):
-            if i == 1:
+            if i >= VECTOR_CHUNKS:
                 nc.scalar.copy(both[i][:, 1, :], token_pairs[1][:, a:b])
             else:
                 nc.vector.tensor_copy(both[i][:, 1, :], token_pairs[1][:, a:b])
@@ -178,7 +203,7 @@ def tile_moe_sdn_lin_relu2_kernel(
         for i, (a, b) in enumerate(TOKEN_CHUNKS):
             dst = quads[i][:].bitcast(F32).rearrange("p (t u) -> p t u", u=2)
             src = both[i][:].rearrange("p u t -> p t u")
-            if i == 1:
+            if i >= VECTOR_CHUNKS:
                 nc.scalar.copy(dst, src)
             else:
                 nc.vector.tensor_copy(dst, src)
@@ -186,7 +211,7 @@ def tile_moe_sdn_lin_relu2_kernel(
             c_codes = keep.tile([P, b - a], U32, name="c_codes%d" % a, align_bytes=64)
             c_scales = keep.tile([P, b - a], U8, name="c_scales%d" % a, align_bytes=64)
             nc.vector.quantize_mx(out=c_codes[:].bitcast(FP8X4), scales=c_scales[:], in_=quads[i][:])
-            product = psum.tile([P, H], F32, tag="sums")
+            product = psum_sums.tile([P, BANK], F32, tag="sums")
             nc.tensor.matmul_mx(
                 out=product[:, : b - a],
                 lhsT=w2_codes[:].bitcast(FP4X4),
@@ -197,7 +222,7 @@ def tile_moe_sdn_lin_relu2_kernel(
                 stop=True,
             )
             result = keep.tile([P, b - a], F32, name="result%d" % a)
-            if i == 2:
+            if i == len(TOKEN_CHUNKS) - 1:
                 nc.vector.tensor_copy(result[:], product[:, : b - a])
             else:
                 nc.scalar.copy(result[:], product[:, : b - a])

@@ -31,7 +31,7 @@ BANK = 512
 GATHER = T // 2
 BANK_STARTS = (0, 2, 6)
 SCATTERS = ((0, 256), (256, 448), (448, 608), (608, 768), (768, 960), (960, 1120), (1120, 1280))
-GPSIMD_COLUMNS = 128
+GPSIMD_COLUMNS = 144
 TOKEN_CHUNKS = ((0, 512), (512, 768), (768, 1024), (1024, 1280))
 VECTOR_CHUNKS = 2
 
@@ -108,8 +108,8 @@ def tile_moe_sdn_lin_relu2_kernel(
             grouped = work.tile([P, b - a, PACK], BF16, align_bytes=64)
             cut = GPSIMD_COLUMNS * (b - a) // H
             nc.scalar.copy(
-                grouped[:, cut:, :].rearrange("p (c i) j -> p c j i", i=4),
-                raw[:, :, cut:].rearrange("p j (c i) -> p c j i", i=4),
+                grouped[:, cut:, :].rearrange("p (c i) j -> p c j i", i=2),
+                raw[:, :, cut:].rearrange("p j (c i) -> p c j i", i=2),
             )
             nc.gpsimd.tensor_scalar(
                 grouped[:, :cut, :], raw[:, :, :cut].rearrange("p j h -> p h j"), 1.0, 0.0, MULT, ADD

from contextlib import ExitStack

import concourse.mybir as mybir
from concourse.masks import make_identity

K, T, E, C, H, N = 1024, 1280, 10, 128, 512, 128
FLOPS = 2 * T * (K * H + H * N)

F32 = mybir.dt.float32
BF16 = mybir.dt.bfloat16
I32 = mybir.dt.int32
U32 = mybir.dt.uint32
U16 = mybir.dt.uint16
U8 = mybir.dt.uint8
FP8X4 = mybir.dt.float8_e4m3fn_x4
FP4X4 = mybir.dt.float4_e2m1fn_x4
MULT = mybir.AluOpType.mult
ADD = mybir.AluOpType.add
MAX = mybir.AluOpType.max
COPY = mybir.ActivationFunctionType.Copy

P = 128
PACK = 4
K_PASS = P * PACK
PASSES = K // K_PASS
QUADRANT = 32
HALF = H // 2
PER_COLUMN = 16
BANK = 512

GATHER = T // 2
BANK_STARTS = (0, 2, 6)
SCATTERS = ((0, 256), (256, 448), (448, 608), (608, 768), (768, 960), (960, 1120), (1120, 1280))
GPSIMD_COLUMNS = 144
TOKEN_CHUNKS = ((0, 512), (512, 768), (768, 1024), (1024, 1280))
VECTOR_CHUNKS = 2


def activation_step(e):
    return PASSES * e + (3 if e < E - 3 else 2)


def tile_moe_sdn_lin_relu2_kernel(
    tc, x_words, x_scales, w1, w2_words, w2_scales, gate, offs, out
):
    nc = tc.nc
    with ExitStack() as ctx:
        keep = ctx.enter_context(tc.tile_pool(name="keep", bufs=1))
        loads = ctx.enter_context(tc.tile_pool(name="loads", bufs=14))
        work = ctx.enter_context(tc.tile_pool(name="work", bufs=4))
        psum_sums = ctx.enter_context(tc.psum_pool(name="psum_sums", bufs=4))
        psum_pairs = ctx.enter_context(tc.psum_pool(name="psum_pairs", bufs=2))

        token_scales = keep.tile([P, T], U8, align_bytes=64)
        nc.vector.memset(token_scales[:].bitcast(I32), 0)
        w2_plane = keep.tile([P, N], U8, align_bytes=64)
        nc.vector.memset(w2_plane[:].bitcast(I32), 0)
        gate_rows = keep.tile([P, C], F32)
        nc.gpsimd.memset(gate_rows[:], 0.0)
        identity = keep.tile([P, P], F32)
        make_identity(nc, identity[:])

        offsets = keep.tile([P, T // PER_COLUMN], U16, name="offsets")
        nc.sync.dma_start(offsets[:], offs)

        def listed(a, b):
            return offsets[:, a // PER_COLUMN : b // PER_COLUMN]

        token_words = [keep.tile([P, T], U32, name="token_words%d" % s, align_bytes=64) for s in range(PASSES)]
        nc.sync.dma_start(token_words[0][:].bitcast(I32), x_words[0].rearrange("p t d -> p (t d)").bitcast(I32))
        for q in range(P // QUADRANT):
            nc.sync.dma_start(
                token_scales[QUADRANT * q : QUADRANT * q + 4 * PASSES, :].bitcast(I32),
                x_scales[:, 4 * q : 4 * q + 4, :].bitcast(I32),
            )
        nc.sync.dma_start(token_words[1][:].bitcast(I32), x_words[1].rearrange("p t d -> p (t d)").bitcast(I32))

        nc.scalar.dma_start(gate_rows[0:E, :], gate[0].rearrange("(e u) -> e u", u=C))
        gate_turned = psum_pairs.tile([P, BANK], F32, tag="pairs0")
        nc.tensor.transpose(gate_turned[:, :P], gate_rows[:], identity[:])
        slot_gate = keep.tile([P, SCATTERS[-2][1] - SCATTERS[-2][0]], F32)
        nc.scalar.copy(slot_gate[:, :16], gate_turned[:, :16])

        slot_words = [keep.tile([P, T], U32, name="slot_words%d" % s, align_bytes=64) for s in range(PASSES)]
        slot_scales = keep.tile([P, T], U8, align_bytes=64)
        for a in range(0, T, GATHER):
            b = a + GATHER
            nc.vector.tensor_copy(slot_words[0][:, a:b], token_words[0][:].indirect(listed(a, b)))
            nc.vector.tensor_copy(slot_scales[:, a:b], token_scales[:].indirect(listed(a, b)))
            nc.vector.tensor_copy(slot_words[1][:, a:b], token_words[1][:].indirect(listed(a, b)))

        token_pairs = [keep.tile([P, T], F32, name="token_pairs%d" % u) for u in range(2)]
        w2_codes = keep.tile([P, 2 * N], U8, align_bytes=64)
        spare = keep.tile([P, 2, H], F32)
        sums = {}
        hidden = {}
        turned = {}

        def bank_start(e):
            return max(f for f in BANK_STARTS if f <= e)

        def multiply(e, s, a, b):
            slots = slice(e * C, (e + 1) * C)
            raw = loads.tile([P, PACK, b - a], F32)
            nc.sync.dma_start(
                raw[:], w1[e, s * K_PASS : (s + 1) * K_PASS, a:b].rearrange("(p j) h -> p j h", j=PACK)
            )
            grouped = work.tile([P, b - a, PACK], BF16, align_bytes=64)
            cut = GPSIMD_COLUMNS * (b - a) // H
            nc.scalar.copy(
                grouped[:, cut:, :].rearrange("p (c i) j -> p c j i", i=2),
                raw[:, :, cut:].rearrange("p j (c i) -> p c j i", i=2),
            )
            nc.gpsimd.tensor_scalar(
                grouped[:, :cut, :], raw[:, :, :cut].rearrange("p j h -> p h j"), 1.0, 0.0, MULT, ADD
            )
            codes = work.tile([P, b - a], U32, align_bytes=64)
            scales = work.tile([P, b - a], U8, align_bytes=64)
            nc.vector.quantize_mx(
                out=codes[:].bitcast(FP8X4), scales=scales[:], in_=grouped[:].rearrange("p h j -> p (h j)")
            )
            width = H if e < E - 1 else HALF
            for c in range(a, b, width):
                if s == 0:
                    sums[e, c] = psum_sums.tile([P, BANK], F32, tag="sums", name="sums")
                nc.tensor.matmul_mx(
                    out=sums[e, c][:, :width],
                    lhsT=slot_words[s][:, slots].bitcast(FP8X4),
                    lhsT_scale=slot_scales[4 * s : P, slots],
                    rhs=codes[:, c - a : c - a + width].bitcast(FP8X4),
                    rhs_scale=scales[:, c - a : c - a + width],
                    start=(s == 0),
                    stop=(s == PASSES - 1),
                )
            return raw

        def activate(e, a, b, gated):
            v = sums[e, a][:, : b - a].rearrange("p (r h) -> p r h", h=HALF)
            nc.scalar.activation(gated, v, COPY, scale=slot_gate[:, e : e + 1])
            nc.vector.scalar_tensor_tensor(
                hidden[e][:, a:b].rearrange("p (r h) -> p r h", h=HALF), v, 0.0, gated, MAX, MULT
            )

        def turn(e):
            first = bank_start(e)
            pairs = hidden[e][:].bitcast(F32)
            for u in range(2):
                if e == first:
                    turned[first, u] = psum_pairs.tile([P, BANK], F32, tag="pairs%d" % u, name="turned")
                nc.tensor.transpose(
                    turned[first, u][:, (e - first) * C : (e - first + 1) * C], pairs[:, u:HALF:2], identity[:]
                )

        def send_back(e, u, room):
            first = bank_start(e)
            for a, b in SCATTERS:
                if e * C < b <= (e + 1) * C:
                    staged = room[:, room.shape[1] - (b - a) :]
                    nc.scalar.copy(staged, turned[first, u][:, a - first * C : b - first * C])
                    nc.vector.tensor_copy(token_pairs[u][:].indirect(listed(a, b)), staged)

        last = E - 1
        pieces = [(e, s, 0, H) for e in range(E) for s in range(PASSES)][:-1]
        pieces.extend([(last, PASSES - 1, 0, HALF), (last, PASSES - 1, HALF, H)])
        for step, piece in enumerate(pieces):
            if step == 4:
                nc.sync.dma_start(w2_codes[:].bitcast(I32), w2_words[0].bitcast(I32))
                for q in range(P // QUADRANT):
                    nc.sync.dma_start(
                        w2_plane[QUADRANT * q : QUADRANT * q + 4, :].bitcast(I32),
                        w2_scales[0, 4 * q : 4 * q + 4, :].bitcast(I32),
                    )
            spent = multiply(*piece)
            due = [e for e in range(last) if activation_step(e) == step]
            for e in due:
                hidden[e] = work.tile([P, H], BF16, name="hidden")
                activate(e, 0, H, spent[:, 0:2, HALF:])
            for e in range(last - 1):
                for u in range(2):
                    if activation_step(e) + 1 + u == step:
                        send_back(e, u, spent[:, 2 + u, :])
            for e in due:
                turn(e)

        hidden[last] = work.tile([P, H], BF16, name="hidden")
        for r in range(2):
            activate(last, r * HALF, (r + 1) * HALF, spare[:, r : r + 1, HALF:])
        send_back(last - 1, 0, spent[:, 0, :])
        send_back(last - 1, 1, slot_gate[:])
        turn(last)
        for u in range(2):
            send_back(last, u, spare[:, u, :HALF])

        both = [keep.tile([P, 2, b - a], F32, name="both%d" % a) for a, b in TOKEN_CHUNKS]
        for i, (a, b) in enumerate(TOKEN_CHUNKS):
            nc.scalar.copy(both[i][:, 0, :], token_pairs[0][:, a:b])
        for i, (a, b) in enumerate(TOKEN_CHUNKS):
            if i >= VECTOR_CHUNKS:
                nc.scalar.copy(both[i][:, 1, :], token_pairs[1][:, a:b])
            else:
                nc.vector.tensor_copy(both[i][:, 1, :], token_pairs[1][:, a:b])
        quads = [keep.tile([P, PACK * (b - a)], BF16, name="quads%d" % a, align_bytes=64) for a, b in TOKEN_CHUNKS]
        for i, (a, b) in enumerate(TOKEN_CHUNKS):
            dst = quads[i][:].bitcast(F32).rearrange("p (t u) -> p t u", u=2)
            src = both[i][:].rearrange("p u t -> p t u")
            if i >= VECTOR_CHUNKS:
                nc.scalar.copy(dst, src)
            else:
                nc.vector.tensor_copy(dst, src)
        for i, (a, b) in enumerate(TOKEN_CHUNKS):
            c_codes = keep.tile([P, b - a], U32, name="c_codes%d" % a, align_bytes=64)
            c_scales = keep.tile([P, b - a], U8, name="c_scales%d" % a, align_bytes=64)
            nc.vector.quantize_mx(out=c_codes[:].bitcast(FP8X4), scales=c_scales[:], in_=quads[i][:])
            product = psum_sums.tile([P, BANK], F32, tag="sums")
            nc.tensor.matmul_mx(
                out=product[:, : b - a],
                lhsT=w2_codes[:].bitcast(FP4X4),
                lhsT_scale=w2_plane[:],
                rhs=c_codes[:].bitcast(FP8X4),
                rhs_scale=c_scales[:],
                start=True,
                stop=True,
            )
            result = keep.tile([P, b - a], F32, name="result%d" % a)
            if i == len(TOKEN_CHUNKS) - 1:
                nc.vector.tensor_copy(result[:], product[:, : b - a])
            else:
                nc.scalar.copy(result[:], product[:, : b - a])
            nc.sync.dma_start(out[:, a:b], result[:])
